import numpy as np
import ml_dtypes


def mxq(x, axis, fmt="e4m3"):
    dtype, down = {"e4m3": (ml_dtypes.float8_e4m3fn, 7), "e5m2": (ml_dtypes.float8_e5m2, 14)}[fmt]
    v = np.moveaxis(np.asarray(x, np.float32).astype(ml_dtypes.bfloat16).astype(np.float64), axis, -1)
    blocks = v.reshape(v.shape[:-1] + (-1, 32))
    amax = np.abs(blocks).max(-1, keepdims=True)
    byte = np.maximum(np.where(amax > 0, np.frexp(amax)[1] - 1 + 127, 0) - down, 1)
    scale = np.exp2(byte - 127.0)
    codes = (blocks / scale).astype(np.float32).astype(dtype).astype(np.float64)
    return np.moveaxis((codes * scale).reshape(v.shape), -1, axis)


WIDE = False


def mx_kscale(k):
    if not WIDE:
        return np.ones(k)
    levels = np.array([10, -10, 5, -5, 0])
    if k % 512:
        return np.exp2(np.random.permutation(np.resize(levels, k // 32))).repeat(32)
    a = np.empty((k // 512, 16))
    for p in range(k // 512):
        a[p, :8] = np.random.permutation(np.resize(levels, 8))
        for g in range(8):
            far = levels[np.abs(levels - a[p, g]) >= 10]
            a[p, g + 8] = far[np.random.randint(len(far))]
    return np.exp2(a.ravel()).repeat(32)


def f64(x):
    return np.asarray(x).astype(np.float64)


def striped(idx):
    return np.tile(idx.reshape(-1, 16).T, (8, 1)).astype(np.uint16)


def unstriped(offs):
    return offs[:16].T.reshape(-1).astype(np.int64)


def striped8(idx):
    return np.concatenate([x.reshape(-1, 16).T for x in idx]).astype(np.uint16)


def runs(offs, k):
    lists = np.stack([offs[16 * r : 16 * r + 16].T.reshape(-1) for r in range(8)]).astype(np.int64)
    return lists[np.arange(k) % 512 // 64]


def pack_weight(w):
    k, n = w.shape
    w = f64(np.asarray(w, np.float32).astype(ml_dtypes.bfloat16)).reshape(k // 32, 32, n)
    amax = np.abs(w).max(1)
    byte = np.clip(np.where(amax > 0, np.frexp(amax)[1] - 1 + 127 - 7, 1), 1, 254)
    scaled = (w * np.exp2(127.0 - byte)[:, None, :]).reshape(k, n).astype(np.float32)
    words = np.ascontiguousarray(scaled.reshape(k // 512, 128, 4, n).transpose(0, 1, 3, 2)).astype(ml_dtypes.float8_e4m3fn).view(np.uint8)
    return words, np.ascontiguousarray(byte.astype(np.uint8).reshape(k // 512, 16, n))


def unpack_weight(words, scales):
    g, p, n, _ = words.shape
    vals = np.ascontiguousarray(words).view(ml_dtypes.float8_e4m3fn).astype(np.float64) * np.repeat(np.exp2(scales.astype(np.float64) - 127.0), 8, axis=1)[..., None]
    return vals.transpose(0, 1, 3, 2).reshape(g * 512, n)


def sigmoid(v):
    return 1.0 / (1.0 + np.exp(-np.maximum(v, -700.0)))

def planes(y):
    n, m = y.shape
    v = y.astype(np.float32).astype(ml_dtypes.bfloat16).astype(np.float64).reshape(n // 32, 32, m)
    top = np.abs(v).max(1)
    byte = np.clip(np.where(top > 0, np.frexp(top)[1] - 1 + 127 - 7, 1), 1, 254)
    codes = (v * np.exp2(127.0 - byte)[:, None, :]).reshape(n, m).astype(np.float32).astype(ml_dtypes.float8_e4m3fn).view(np.uint8)
    words = codes.reshape(n // 512, 128, 4, m).transpose(0, 1, 3, 2)
    return np.ascontiguousarray(words), np.ascontiguousarray(byte.astype(np.uint8).reshape(n // 512, 16, m))


K, T, S, H = 512, 2048, 512, 512


def setup_inputs():
    n = np.random.standard_normal
    s = mx_kscale(K)[:, None]
    u = mx_kscale(S)
    packed_xT = pack_weight(n((K, T)) * s)
    packed_w1 = pack_weight(n((K, H)) / np.sqrt(K) / s)
    return {
        "x_words": packed_xT[0],
        "x_scales": packed_xT[1],
        "w1_words": packed_w1[0],
        "w1_scales": packed_w1[1],
        "ga": (np.random.uniform(0.5, 1.5, (H, 1)) * u[:, None]).astype(np.float32),
        "gb": (np.random.uniform(0.5, 1.5, (H, 1)) / u[:, None]).astype(np.float32),
        "offs": striped(np.random.permutation(T)[:S]),
        "n1": striped8(np.stack([np.random.permutation(S) for _ in range(8)])),
        "n2": striped8(np.stack([np.random.permutation(S) for _ in range(8)])),
        "n3": striped8(np.stack([np.random.permutation(S) for _ in range(8)])),
        "n4": striped8(np.stack([np.random.permutation(S) for _ in range(8)])),
        "n5": striped8(np.stack([np.random.permutation(S) for _ in range(8)])),
    }


def reference(x_words, x_scales, w1_words, w1_scales, ga, gb, offs, n1, n2, n3, n4, n5):
    xq = unpack_weight(x_words, x_scales)[:, unstriped(offs)]
    y = unpack_weight(w1_words, w1_scales).T @ xq
    st = y - (y[np.arange(H)[:, None], runs(n1, H)])
    z = f64(ga) * (np.maximum(st, st[np.arange(H)[:, None], runs(n2, H)]))
    z2 = f64(gb) * (y + (sigmoid(y[np.arange(H)[:, None], runs(n3, H)])) * (y[np.arange(H)[:, None], runs(n4, H)] - y))
    s = 0.0625 * ((mxq(z, 0, "e4m3").T @ mxq(z2, 0, "e4m3")))
    pa = s[np.arange(S)[:, None], runs(n5, S)]
    out_0 = (2.0 * (s * pa)) / ((s) ** 2 + (pa) ** 2 + 0.5)
    return (out_0,) + planes(out_0)

@@ -1,0 +1,233 @@
+from contextlib import ExitStack
+
+import concourse.mybir as mybir
+
+F32 = mybir.dt.float32
+BF16 = mybir.dt.bfloat16
+I32 = mybir.dt.int32
+U32 = mybir.dt.uint32
+U16 = mybir.dt.uint16
+U8 = mybir.dt.uint8
+FP8X4 = mybir.dt.float8_e4m3fn_x4
+ALU = mybir.AluOpType
+ACT = mybir.ActivationFunctionType
+
+P = 128
+PACK = 4
+T = 2048
+S = 512
+HALF = S // 2
+WIDE = 2 * S
+FLOPS = 2 * 2 * 512 * 512 * 512
+
+
+def tile_picked_selfhopmxtrackharm_none_po_kernel(
+    tc, x_words, x_scales, w1_words, w1_scales, ga, gb, offs, n1, n2, n3, n4, n5, out_0, out_1, out_2
+):
+    nc = tc.nc
+    with ExitStack() as ctx:
+        held = ctx.enter_context(tc.tile_pool(name="held", bufs=1))
+        psum = ctx.enter_context(tc.psum_pool(name="psum", bufs=1))
+
+        def new(name, shape, dtype):
+            return held.tile(shape, dtype, name=name, align_bytes=64)
+
+        lists = {}
+        for name in ("offs", "n1", "n2", "n3", "n4", "n5"):
+            lists[name] = held.tile([P, S // 16], U16, name="list_" + name)
+
+        xw = new("xw", [P, T], I32)
+        xs = new("xs", [P, T], U8)
+        ww = new("ww", [P, S], I32)
+        ws = new("ws", [P, S], U8)
+        ga_t = new("ga_t", [P, PACK], F32)
+        gb_t = new("gb_t", [P, PACK], F32)
+        warm_in = new("warm_in", [P, 1], F32)
+        warm_a = new("warm_a", [P, 1], F32)
+        warm_b = new("warm_b", [P, 1], F32)
+
+        nc.vector.memset(xs[:].bitcast(I32), 0)
+        nc.gpsimd.memset(ws[:].bitcast(I32), 0)
+        nc.vector.memset(warm_in[:], 0.0)
+        nc.sync.dma_start(lists["offs"][:], offs)
+        for q in range(4):
+            nc.sync.dma_start(xs[32 * q : 32 * q + 4, :].bitcast(I32), x_scales[0, 4 * q : 4 * q + 4, :].bitcast(I32))
+        nc.sync.dma_start(xw[:], x_words[0].rearrange("p c r -> p (c r)").bitcast(I32))
+        for q in range(4):
+            nc.scalar.dma_start(ws[32 * q : 32 * q + 4, :].bitcast(I32), w1_scales[0, 4 * q : 4 * q + 4, :].bitcast(I32))
+        nc.scalar.dma_start(ww[:], w1_words[0].rearrange("p c r -> p (c r)").bitcast(I32))
+        nc.gpsimd.dma_start(ga_t[:], ga.rearrange("(p t) o -> p (t o)", t=PACK))
+        nc.scalar.activation(warm_a[:], warm_in[:], ACT.Sigmoid)
+        nc.gpsimd.dma_start(gb_t[:], gb.rearrange("(p t) o -> p (t o)", t=PACK))
+        for name, src in (("n1", n1), ("n2", n2), ("n3", n3), ("n4", n4), ("n5", n5)):
+            nc.sync.dma_start(lists[name][:], src)
+
+        xgw = new("xgw", [P, S], I32)
+        xgs = new("xgs", [P, S], U8)
+        nc.vector.tensor_copy(xgs[:], xs[:].indirect(lists["offs"][:]))
+        wdw = new("wdw", [P, PACK, P], I32)
+        wds = new("wds", [P, PACK, P], U8)
+        nc.vector.tensor_copy(wds[:].rearrange("p t m -> p m t"), ws[:].rearrange("p (m t) -> p m t", t=PACK))
+        nc.vector.tensor_copy(
+            wdw[:].bitcast(U32).rearrange("p t m -> p m t"), ww[:].bitcast(U32).rearrange("p (m t) -> p m t", t=PACK)
+        )
+        flip = new("flip", [P, PACK], F32)
+        nga = new("nga", [P, PACK], F32)
+        ngb = new("ngb", [P, PACK], F32)
+        nc.vector.tensor_scalar(flip[:], ga_t[:], 0.0, -2.0, ALU.is_ge, ALU.mult)
+        nc.vector.scalar_tensor_tensor(nga[:], flip[:], 1.0, ga_t[:], ALU.add, ALU.mult)
+        nc.vector.scalar_tensor_tensor(ngb[:], flip[:], 1.0, gb_t[:], ALU.add, ALU.mult)
+        nc.vector.tensor_copy(xgw[:].bitcast(U32), xw[:].bitcast(U32).indirect(lists["offs"][:]))
+
+        y_ps = [psum.tile([P, S], F32, name="y_ps%d" % t, tag="bank%d" % t) for t in range(PACK)]
+        for t in range(PACK):
+            nc.tensor.matmul_mx(
+                y_ps[t][:], lhsT=wdw[:, t, :].bitcast(FP8X4), lhsT_scale=wds[:, t, :],
+                rhs=xgw[:].bitcast(FP8X4), rhs_scale=xgs[:], start=True, stop=True,
+            )
+
+        ya_win = [new("ya_win%d" % t, [P, WIDE], F32) for t in range(PACK)]
+        y_win = [new("y_win%d" % t, [P, WIDE], F32) for t in range(PACK)]
+        yb_win = [new("yb_win%d" % t, [P, WIDE], F32) for t in range(PACK)]
+        st_win = [new("st_win%d" % t, [P, WIDE], F32) for t in range(PACK)]
+        ya = [new("ya%d" % t, [P, S], F32) for t in range(PACK)]
+        st_hop = [new("st_hop%d" % t, [P, S], F32) for t in range(PACK)]
+        gate = [new("gate%d" % t, [P, S], F32) for t in range(PACK)]
+        far = new("far", [P, PACK, S], F32)
+        near = new("near", [P, PACK, S], F32)
+        z_planes = new("z_planes", [P, PACK, PACK, P], BF16)
+        z_il = new("z_il", [P, PACK, P, PACK], BF16)
+        z2_il = new("z2_il", [P, S, PACK], BF16)
+        z_w = new("z_w", [P, S], U32)
+        z_s = new("z_s", [P, S], U8)
+        z2_w = new("z2_w", [P, S], U32)
+        z2_s = new("z2_s", [P, S], U8)
+
+        def evict_a(t):
+            nc.scalar.activation(ya_win[t][:, :S], y_ps[t][:], ACT.Copy, scale=nga[:, t : t + 1])
+            nc.scalar.activation(ya[t][:], y_ps[t][:], ACT.Copy, scale=nga[:, t : t + 1])
+
+        def evict_b(t):
+            nc.scalar.copy(y_win[t][:, :S], y_ps[t][:])
+            nc.scalar.activation(gate[t][:], y_win[t][:].indirect(lists["n3"][:]), ACT.Sigmoid)
+            nc.scalar.activation(yb_win[t][:, :S], y_ps[t][:], ACT.Copy, scale=ngb[:, t : t + 1])
+
+        def step_a(t):
+            nc.vector.tensor_tensor(st_win[t][:, :S], ya_win[t][:].indirect(lists["n1"][:]), ya[t][:], ALU.subtract)
+
+        def step_b(t):
+            nc.vector.tensor_copy(st_hop[t][:], st_win[t][:].indirect(lists["n2"][:]))
+
+        def step_c(t):
+            nc.vector.tensor_tensor(
+                z_planes[:, t].rearrange("p u m -> p m u"),
+                st_win[t][:, :S].rearrange("p (m u) -> p m u", u=PACK),
+                st_hop[t][:].rearrange("p (m u) -> p m u", u=PACK),
+                ALU.max,
+            )
+
+        def step_d(t):
+            nc.vector.tensor_tensor(far[:, t, :], yb_win[t][:].indirect(lists["n4"][:]), gate[t][:], ALU.mult)
+
+        def step_e(t):
+            nc.vector.scalar_tensor_tensor(near[:, t, :], gate[t][:], 1.0, yb_win[t][:, :S], ALU.subtract, ALU.mult)
+
+        evict_a(0)
+        step_a(0)
+        step_b(0)
+        step_c(0)
+        for t in range(1, PACK):
+            evict_a(t)
+            evict_b(t - 1)
+            step_a(t)
+            step_d(t - 1)
+            step_b(t)
+            step_e(t - 1)
+            step_c(t)
+        evict_b(PACK - 1)
+        nc.scalar.activation(warm_b[:], gate[PACK - 1][:, 0:1], ACT.Abs_reciprocal_sqrt)
+        for u in range(PACK):
+            nc.scalar.copy(
+                z_il[:, u].rearrange("p (c i) t -> p c t i", i=4),
+                z_planes[:, :, u, :].rearrange("p t (c i) -> p c t i", i=4),
+            )
+        step_d(PACK - 1)
+        step_e(PACK - 1)
+
+        s_ps = [[None] * PACK, [None] * PACK]
+        s_win = [new("s_win%d" % u, [P, S], F32) for u in range(PACK)]
+        s_sq = [new("s_sq%d" % h, [P, PACK, HALF], F32) for h in range(2)]
+        for h in range(2):
+            cols = slice(h * HALF, (h + 1) * HALF)
+            nc.vector.tensor_tensor(
+                z2_il[:, cols, :].rearrange("p (c i) t -> p c t i", i=4),
+                near[:, :, cols].rearrange("p t (c i) -> p c t i", i=4),
+                far[:, :, cols].rearrange("p t (c i) -> p c t i", i=4),
+                ALU.subtract,
+            )
+            if h == 0:
+                nc.vector.quantize_mx(z_w[:].bitcast(FP8X4), z_s[:], z_il[:].rearrange("p u m t -> p (u m t)"))
+            nc.vector.quantize_mx(z2_w[:, cols].bitcast(FP8X4), z2_s[:, cols], z2_il[:, cols, :].rearrange("p j t -> p (j t)"))
+            for u in range(PACK):
+                bank = u + PACK * (1 - h)
+                s_ps[h][u] = psum.tile([P, HALF], F32, name="s_ps%d%d" % (h, u), tag="bank%d" % bank)
+                nc.tensor.matmul_mx(
+                    s_ps[h][u][:], lhsT=z_w[:, u * P : (u + 1) * P].bitcast(FP8X4), lhsT_scale=z_s[:, u * P : (u + 1) * P],
+                    rhs=z2_w[:, cols].bitcast(FP8X4), rhs_scale=z2_s[:, cols], start=True, stop=True,
+                )
+            for u in range(PACK):
+                nc.scalar.activation(s_win[u][:, cols], s_ps[h][u][:], ACT.Copy, scale=0.0625)
+
+        pa = [new("pa%d" % h, [P, PACK, HALF], F32) for h in range(2)]
+        pa_sq = [new("pa_sq%d" % h, [P, PACK, HALF], F32) for h in range(2)]
+        num = [new("num%d" % h, [P, PACK, HALF], F32) for h in range(2)]
+        den = [new("den%d" % h, [P, PACK, HALF], F32) for h in range(2)]
+        root = [new("root%d" % h, [P, PACK, HALF], F32) for h in range(2)]
+        inv = [new("inv%d" % h, [P, PACK, HALF], F32) for h in range(2)]
+        res = [new("res%d" % h, [P, PACK, HALF], F32) for h in range(2)]
+        res_il = [new("res_il%d" % h, [P, HALF, PACK], BF16) for h in range(2)]
+        res_w = new("res_w", [P, S], I32)
+        res_s = new("res_s", [P, S], U8)
+        out_rows = out_0.rearrange("(p t) c -> p t c", t=PACK)
+        out_words = out_1[0].rearrange("p c r -> p (c r)").bitcast(I32)
+
+        def front(h, v):
+            us = slice(2 * v, 2 * v + 2)
+            for u in (2 * v, 2 * v + 1):
+                nc.scalar.activation(s_sq[h][:, u, :], s_ps[h][u][:], ACT.Square, scale=0.0625)
+            for u in (2 * v, 2 * v + 1):
+                nc.vector.tensor_copy(pa[h][:, u, :], s_win[u][:].indirect(lists["n5"][:, 16 * h : 16 * h + 16]))
+            nc.scalar.activation(pa_sq[h][:, us, :], pa[h][:, us, :], ACT.Square)
+            for u in (2 * v, 2 * v + 1):
+                nc.vector.scalar_tensor_tensor(num[h][:, u, :], s_ps[h][u][:], 0.125, pa[h][:, u, :], ALU.mult, ALU.mult)
+
+        def middle(h, v):
+            us = slice(2 * v, 2 * v + 2)
+            nc.vector.scalar_tensor_tensor(den[h][:, us, :], s_sq[h][:, us, :], 0.5, pa_sq[h][:, us, :], ALU.add, ALU.add)
+            nc.scalar.activation(root[h][:, us, :], den[h][:, us, :], ACT.Abs_reciprocal_sqrt)
+            nc.scalar.activation(inv[h][:, us, :], root[h][:, us, :], ACT.Square)
+
+        def back(h, v):
+            us = slice(2 * v, 2 * v + 2)
+            cols = slice(h * HALF, (h + 1) * HALF)
+            nc.vector.tensor_tensor(res[h][:, us, :], num[h][:, us, :], inv[h][:, us, :], ALU.mult)
+            nc.sync.dma_start(out_rows[:, us, cols], res[h][:, us, :])
+            if v == 1:
+                nc.vector.tensor_copy(
+                    res_il[h][:].rearrange("p (c i) t -> p c t i", i=4),
+                    res[h][:].rearrange("p t (c i) -> p c t i", i=4),
+                )
+                nc.vector.quantize_mx(res_w[:, cols].bitcast(FP8X4), res_s[:, cols], res_il[h][:].rearrange("p j t -> p (j t)"))
+                nc.sync.dma_start(out_words[:, cols], res_w[:, cols])
+
+        units = [(h, v) for h in range(2) for v in range(2)]
+        for i in range(len(units) + 2):
+            if i < len(units):
+                front(*units[i])
+            if 1 <= i <= len(units):
+                middle(*units[i - 1])
+            if i >= 2:
+                back(*units[i - 2])
+        for q in range(4):
+            eng = nc.scalar if q % 2 else nc.sync
+            eng.dma_start(out_2[0, 4 * q : 4 * q + 4, :].bitcast(I32), res_s[32 * q : 32 * q + 4, :].bitcast(I32))

@@ -1,6 +1,7 @@
 from contextlib import ExitStack
 
 import concourse.mybir as mybir
+from concourse.masks import make_identity
 
 F32 = mybir.dt.float32
 BF16 = mybir.dt.bfloat16
@@ -29,8 +30,8 @@ def tile_picked_selfhopmxtrackharm_none_po_kernel(
         held = ctx.enter_context(tc.tile_pool(name="held", bufs=1))
         psum = ctx.enter_context(tc.psum_pool(name="psum", bufs=1))
 
-        def new(name, shape, dtype):
-            return held.tile(shape, dtype, name=name, align_bytes=64)
+        def new(name, shape, dtype, tag=""):
+            return held.tile(shape, dtype, name=name, tag=tag or name, align_bytes=64)
 
         lists = {}
         for name in ("offs", "n1", "n2", "n3", "n4", "n5"):
@@ -46,188 +47,262 @@ def tile_picked_selfhopmxtrackharm_none_po_kernel(
         warm_a = new("warm_a", [P, 1], F32)
         warm_b = new("warm_b", [P, 1], F32)
 
-        nc.vector.memset(xs[:].bitcast(I32), 0)
+        nc.gpsimd.memset(xs[:].bitcast(I32), 0)
         nc.gpsimd.memset(ws[:].bitcast(I32), 0)
         nc.vector.memset(warm_in[:], 0.0)
-        nc.sync.dma_start(lists["offs"][:], offs)
-        for q in range(4):
-            nc.sync.dma_start(xs[32 * q : 32 * q + 4, :].bitcast(I32), x_scales[0, 4 * q : 4 * q + 4, :].bitcast(I32))
-        nc.sync.dma_start(xw[:], x_words[0].rearrange("p c r -> p (c r)").bitcast(I32))
-        for q in range(4):
-            nc.scalar.dma_start(ws[32 * q : 32 * q + 4, :].bitcast(I32), w1_scales[0, 4 * q : 4 * q + 4, :].bitcast(I32))
-        nc.scalar.dma_start(ww[:], w1_words[0].rearrange("p c r -> p (c r)").bitcast(I32))
-        nc.gpsimd.dma_start(ga_t[:], ga.rearrange("(p t) o -> p (t o)", t=PACK))
-        nc.scalar.activation(warm_a[:], warm_in[:], ACT.Sigmoid)
-        nc.gpsimd.dma_start(gb_t[:], gb.rearrange("(p t) o -> p (t o)", t=PACK))
-        for name, src in (("n1", n1), ("n2", n2), ("n3", n3), ("n4", n4), ("n5", n5)):
+
+        def scale_rows(dst, src, queues):
+            for q, eng in enumerate(queues):
+                eng.dma_start(dst[32 * q : 32 * q + 4, :].bitcast(I32), src[0, 4 * q : 4 * q + 4, :].bitcast(I32))
+
+        nc.scalar.dma_start(ga_t[:], ga.rearrange("(p t) o -> p (t o)", t=PACK))
+        for name, src in (("offs", offs), ("n1", n1), ("n2", n2)):
             nc.sync.dma_start(lists[name][:], src)
+        nc.sync.dma_start(xw[:], x_words[0].rearrange("p c r -> p (c r)").bitcast(I32))
+        scale_rows(xs, x_scales, [nc.sync] * 4)
+        scale_rows(ws, w1_scales, [nc.sync, nc.sync, nc.gpsimd, nc.gpsimd])
+        nc.sync.dma_start(ww[:], w1_words[0].rearrange("p c r -> p (c r)").bitcast(I32))
+        nc.sync.dma_start(gb_t[:], gb.rearrange("(p t) o -> p (t o)", t=PACK))
+        for name, src in (("n3", n3), ("n4", n4), ("n5", n5)):
+            nc.sync.dma_start(lists[name][:], src)
+        nc.scalar.activation(warm_a[:], warm_in[:], ACT.Sigmoid)
+        ident = new("ident", [P, P], F32)
+        make_identity(nc, ident[:])
 
         xgw = new("xgw", [P, S], I32)
         xgs = new("xgs", [P, S], U8)
-        nc.vector.tensor_copy(xgs[:], xs[:].indirect(lists["offs"][:]))
-        wdw = new("wdw", [P, PACK, P], I32)
-        wds = new("wds", [P, PACK, P], U8)
-        nc.vector.tensor_copy(wds[:].rearrange("p t m -> p m t"), ws[:].rearrange("p (m t) -> p m t", t=PACK))
-        nc.vector.tensor_copy(
-            wdw[:].bitcast(U32).rearrange("p t m -> p m t"), ww[:].bitcast(U32).rearrange("p (m t) -> p m t", t=PACK)
-        )
+        wdw = [new("wdw%d" % t, [P, P], I32) for t in range(PACK)]
+        wds = [new("wds%d" % t, [P, P], U8) for t in range(PACK)]
         flip = new("flip", [P, PACK], F32)
-        nga = new("nga", [P, PACK], F32)
+        aga = new("aga", [P, PACK], F32)
         ngb = new("ngb", [P, PACK], F32)
-        nc.vector.tensor_scalar(flip[:], ga_t[:], 0.0, -2.0, ALU.is_ge, ALU.mult)
-        nc.vector.scalar_tensor_tensor(nga[:], flip[:], 1.0, ga_t[:], ALU.add, ALU.mult)
-        nc.vector.scalar_tensor_tensor(ngb[:], flip[:], 1.0, gb_t[:], ALU.add, ALU.mult)
+        nc.scalar.activation(aga[:], ga_t[:], ACT.Abs)
+        ww_by_t = ww[:].bitcast(U32).rearrange("p (m t) -> p m t", t=PACK)
+        ws_by_t = ws[:].rearrange("p (m t) -> p m t", t=PACK)
         nc.vector.tensor_copy(xgw[:].bitcast(U32), xw[:].bitcast(U32).indirect(lists["offs"][:]))
+        nc.vector.tensor_copy(xgs[:, :HALF], xs[:].indirect(lists["offs"][:, :16]))
+        nc.vector.tensor_copy(wdw[0][:].bitcast(U32), ww_by_t[:, :, 0])
+        nc.vector.tensor_copy(wds[0][:], ws_by_t[:, :, 0])
+        nc.vector.tensor_copy(xgs[:, HALF:], xs[:].indirect(lists["offs"][:, 16:]))
+        for t in range(1, PACK):
+            nc.vector.tensor_copy(wdw[t][:].bitcast(U32), ww_by_t[:, :, t])
+            nc.vector.tensor_copy(wds[t][:], ws_by_t[:, :, t])
+        nc.vector.tensor_scalar(flip[:], ga_t[:], 0.0, -2.0, ALU.is_ge, ALU.mult)
+        nc.vector.scalar_tensor_tensor(ngb[:], flip[:], 1.0, gb_t[:], ALU.add, ALU.mult)
 
-        y_ps = [psum.tile([P, S], F32, name="y_ps%d" % t, tag="bank%d" % t) for t in range(PACK)]
+        y_parts = []
         for t in range(PACK):
-            nc.tensor.matmul_mx(
-                y_ps[t][:], lhsT=wdw[:, t, :].bitcast(FP8X4), lhsT_scale=wds[:, t, :],
-                rhs=xgw[:].bitcast(FP8X4), rhs_scale=xgs[:], start=True, stop=True,
-            )
+            spans = ((slice(0, HALF), 0), (slice(HALF, S), PACK)) if t == 0 else ((slice(0, S), t),)
+            parts = []
+            for cols, bank in spans:
+                acc = psum.tile([P, cols.stop - cols.start], F32, name="y_ps%d" % bank, tag="bank%d" % bank)
+                nc.tensor.matmul_mx(
+                    acc[:], lhsT=wdw[t][:].bitcast(FP8X4), lhsT_scale=wds[t][:],
+                    rhs=xgw[:, cols].bitcast(FP8X4), rhs_scale=xgs[:, cols], start=True, stop=True,
+                )
+                parts.append((cols, acc))
+            y_parts.append(parts)
 
         ya_win = [new("ya_win%d" % t, [P, WIDE], F32) for t in range(PACK)]
         y_win = [new("y_win%d" % t, [P, WIDE], F32) for t in range(PACK)]
         yb_win = [new("yb_win%d" % t, [P, WIDE], F32) for t in range(PACK)]
-        st_win = [new("st_win%d" % t, [P, WIDE], F32) for t in range(PACK)]
+        st_win = [new("st_win%d" % t, [P, S], F32) for t in range(PACK)]
         ya = [new("ya%d" % t, [P, S], F32) for t in range(PACK)]
-        st_hop = [new("st_hop%d" % t, [P, S], F32) for t in range(PACK)]
+        st_hop = [[new("st_hop%d%d" % (t, h), [P, HALF], F32) for h in range(2)] for t in range(PACK)]
         gate = [new("gate%d" % t, [P, S], F32) for t in range(PACK)]
-        far = new("far", [P, PACK, S], F32)
-        near = new("near", [P, PACK, S], F32)
-        z_planes = new("z_planes", [P, PACK, PACK, P], BF16)
-        z_il = new("z_il", [P, PACK, P, PACK], BF16)
+        far = [new("far%d" % t, [P, S], F32) for t in range(PACK)]
+        near = [new("near%d" % t, [P, S], F32) for t in range(PACK)]
+        z_planes = new("z_planes", [P, PACK, S], BF16)
+        z2_turned = [new("z2_turned%d" % b, [P, 2, P, 2], BF16) for b in range(PACK)]
         z2_il = new("z2_il", [P, S, PACK], BF16)
-        z_w = new("z_w", [P, S], U32)
-        z_s = new("z_s", [P, S], U8)
+        z_w = [new("z_w%d" % u, [P, P], U32) for u in range(PACK)]
+        z_s = [new("z_s%d" % u, [P, P], U8) for u in range(PACK)]
         z2_w = new("z2_w", [P, S], U32)
         z2_s = new("z2_s", [P, S], U8)
+        sum_ps = [psum.tile([P, PACK, P], F32, name="sum_ps%d" % b, tag="bank%d" % (PACK + b)) for b in range(PACK)]
 
         def evict_a(t):
-            nc.scalar.activation(ya_win[t][:, :S], y_ps[t][:], ACT.Copy, scale=nga[:, t : t + 1])
-            nc.scalar.activation(ya[t][:], y_ps[t][:], ACT.Copy, scale=nga[:, t : t + 1])
+            for cols, acc in y_parts[t]:
+                nc.scalar.activation(ya_win[t][:, cols], acc[:], ACT.Copy, scale=aga[:, t : t + 1])
+                nc.scalar.activation(ya[t][:, cols], acc[:], ACT.Copy, scale=aga[:, t : t + 1])
 
         def evict_b(t):
-            nc.scalar.copy(y_win[t][:, :S], y_ps[t][:])
+            for cols, acc in y_parts[t]:
+                nc.scalar.copy(y_win[t][:, cols], acc[:])
+            for cols, acc in y_parts[t]:
+                nc.scalar.activation(yb_win[t][:, cols], acc[:], ACT.Copy, scale=ngb[:, t : t + 1])
+
+        def make_gate(t):
             nc.scalar.activation(gate[t][:], y_win[t][:].indirect(lists["n3"][:]), ACT.Sigmoid)
-            nc.scalar.activation(yb_win[t][:, :S], y_ps[t][:], ACT.Copy, scale=ngb[:, t : t + 1])
 
         def step_a(t):
             nc.vector.tensor_tensor(st_win[t][:, :S], ya_win[t][:].indirect(lists["n1"][:]), ya[t][:], ALU.subtract)
 
         def step_b(t):
-            nc.vector.tensor_copy(st_hop[t][:], st_win[t][:].indirect(lists["n2"][:]))
+            for h in range(2):
+                nc.vector.tensor_copy(st_hop[t][h][:], st_win[t][:].indirect(lists["n2"][:, 16 * h : 16 * h + 16]))
 
         def step_c(t):
-            nc.vector.tensor_tensor(
-                z_planes[:, t].rearrange("p u m -> p m u"),
-                st_win[t][:, :S].rearrange("p (m u) -> p m u", u=PACK),
-                st_hop[t][:].rearrange("p (m u) -> p m u", u=PACK),
-                ALU.max,
-            )
+            for h in range(2):
+                cols = slice(h * HALF, (h + 1) * HALF)
+                nc.vector.tensor_tensor(z_planes[:, t, cols], st_win[t][:, cols], st_hop[t][h][:], ALU.min)
 
         def step_d(t):
-            nc.vector.tensor_tensor(far[:, t, :], yb_win[t][:].indirect(lists["n4"][:]), gate[t][:], ALU.mult)
+            nc.vector.tensor_tensor(far[t][:], yb_win[t][:].indirect(lists["n4"][:]), gate[t][:], ALU.mult)
 
         def step_e(t):
-            nc.vector.scalar_tensor_tensor(near[:, t, :], gate[t][:], 1.0, yb_win[t][:, :S], ALU.subtract, ALU.mult)
+            nc.vector.scalar_tensor_tensor(near[t][:], gate[t][:], -1.0, yb_win[t][:, :S], ALU.mult, ALU.mult)
+            terms = (yb_win[t], far[t], near[t])
+            for i, term in enumerate(terms):
+                for b in range(PACK):
+                    nc.tensor.matmul(
+                        sum_ps[b][:, t, :], lhsT=term[:, b * P : (b + 1) * P], rhs=ident[:],
+                        is_transpose=True, start=(i == 0), stop=(i == len(terms) - 1),
+                    )
 
         evict_a(0)
+        evict_b(0)
+        make_gate(0)
+        evict_b(1)
+        evict_a(1)
+        make_gate(1)
+        evict_b(2)
+        make_gate(2)
+        evict_b(3)
+        evict_a(2)
+        make_gate(3)
+        evict_a(3)
+        nc.scalar.activation(warm_b[:], ya[3][:, S - 1 : S], ACT.Abs_reciprocal_sqrt, scale=0.0, bias=1.0)
         step_a(0)
         step_b(0)
         step_c(0)
-        for t in range(1, PACK):
-            evict_a(t)
-            evict_b(t - 1)
-            step_a(t)
-            step_d(t - 1)
-            step_b(t)
-            step_e(t - 1)
-            step_c(t)
-        evict_b(PACK - 1)
-        nc.scalar.activation(warm_b[:], gate[PACK - 1][:, 0:1], ACT.Abs_reciprocal_sqrt)
-        for u in range(PACK):
-            nc.scalar.copy(
-                z_il[:, u].rearrange("p (c i) t -> p c t i", i=4),
-                z_planes[:, :, u, :].rearrange("p t (c i) -> p c t i", i=4),
-            )
-        step_d(PACK - 1)
-        step_e(PACK - 1)
+        step_d(0)
+        step_e(0)
+        step_a(1)
+        step_d(1)
+        step_b(1)
+        step_e(1)
+        step_c(1)
+        step_d(2)
+        step_e(2)
+        step_a(2)
+        step_d(3)
+        step_e(3)
+        step_b(2)
+        step_a(3)
+        step_c(2)
+        step_b(3)
 
-        s_ps = [[None] * PACK, [None] * PACK]
-        s_win = [new("s_win%d" % u, [P, S], F32) for u in range(PACK)]
-        s_sq = [new("s_sq%d" % h, [P, PACK, HALF], F32) for h in range(2)]
+        back_ps = [psum.tile([P, 2, 2, P], F32, name="back_ps%d" % h, tag="bank%d" % h) for h in range(2)]
         for h in range(2):
-            cols = slice(h * HALF, (h + 1) * HALF)
-            nc.vector.tensor_tensor(
-                z2_il[:, cols, :].rearrange("p (c i) t -> p c t i", i=4),
-                near[:, :, cols].rearrange("p t (c i) -> p c t i", i=4),
-                far[:, :, cols].rearrange("p t (c i) -> p c t i", i=4),
-                ALU.subtract,
-            )
-            if h == 0:
-                nc.vector.quantize_mx(z_w[:].bitcast(FP8X4), z_s[:], z_il[:].rearrange("p u m t -> p (u m t)"))
-            nc.vector.quantize_mx(z2_w[:, cols].bitcast(FP8X4), z2_s[:, cols], z2_il[:, cols, :].rearrange("p j t -> p (j t)"))
-            for u in range(PACK):
-                bank = u + PACK * (1 - h)
-                s_ps[h][u] = psum.tile([P, HALF], F32, name="s_ps%d%d" % (h, u), tag="bank%d" % bank)
-                nc.tensor.matmul_mx(
-                    s_ps[h][u][:], lhsT=z_w[:, u * P : (u + 1) * P].bitcast(FP8X4), lhsT_scale=z_s[:, u * P : (u + 1) * P],
-                    rhs=z2_w[:, cols].bitcast(FP8X4), rhs_scale=z2_s[:, cols], start=True, stop=True,
-                )
-            for u in range(PACK):
-                nc.scalar.activation(s_win[u][:, cols], s_ps[h][u][:], ACT.Copy, scale=0.0625)
+            for b in (2 * h, 2 * h + 1):
+                nc.scalar.copy(z2_turned[b][:], sum_ps[b][:].rearrange("j (u e) p -> j u p e", e=2))
+                words = z2_turned[b][:].rearrange("j u p e -> j (u p e)").bitcast(F32)
+                for u in range(2):
+                    nc.tensor.transpose(back_ps[h][:, b % 2, u, :], words[:, u * P : (u + 1) * P], ident[:])
+        for h in range(2):
+            dst = z2_il[:, h * HALF : (h + 1) * HALF, :].rearrange("p j t -> p (j t)").bitcast(F32)
+            nc.scalar.copy(dst.rearrange("p (b j u) -> p b j u", b=2, u=2), back_ps[h][:].rearrange("p b u j -> p b j u"))
+        step_c(3)
 
-        pa = [new("pa%d" % h, [P, PACK, HALF], F32) for h in range(2)]
-        pa_sq = [new("pa_sq%d" % h, [P, PACK, HALF], F32) for h in range(2)]
-        num = [new("num%d" % h, [P, PACK, HALF], F32) for h in range(2)]
-        den = [new("den%d" % h, [P, PACK, HALF], F32) for h in range(2)]
-        root = [new("root%d" % h, [P, PACK, HALF], F32) for h in range(2)]
-        inv = [new("inv%d" % h, [P, PACK, HALF], F32) for h in range(2)]
-        res = [new("res%d" % h, [P, PACK, HALF], F32) for h in range(2)]
-        res_il = [new("res_il%d" % h, [P, HALF, PACK], BF16) for h in range(2)]
+        z_il = [new("z_il%d" % u, [P, P, PACK], BF16, tag="z2_turned3" if u == 1 else "z2_turned2" if u == 2 else "") for u in range(PACK)]
+
+        def weave(copy, u):
+            copy(
+                z_il[u][:].rearrange("p (c i) t -> p c t i", i=4),
+                z_planes[:].rearrange("p t (c i u) -> p u c t i", i=4, u=PACK)[:, u],
+            )
+
+        s_ps = [psum.tile([P, S], F32, name="s_ps%d" % u, tag="bank%d" % (2 + u)) for u in range(PACK)]
+        s_win = [new("s_win%d" % u, [P, WIDE], F32) for u in range(PACK)]
+        s_sq = new("s_sq", [P, PACK, S], F32)
+
+        def product(u):
+            nc.vector.quantize_mx(z_w[u][:].bitcast(FP8X4), z_s[u][:], z_il[u][:].rearrange("p m t -> p (m t)"))
+            nc.tensor.matmul_mx(
+                s_ps[u][:], lhsT=z_w[u][:].bitcast(FP8X4), lhsT_scale=z_s[u][:],
+                rhs=z2_w[:].bitcast(FP8X4), rhs_scale=z2_s[:], start=True, stop=True,
+            )
+
+        weave(nc.vector.tensor_copy, 0)
+        nc.vector.quantize_mx(z2_w[:].bitcast(FP8X4), z2_s[:], z2_il[:].rearrange("p j t -> p (j t)"))
+        weave(nc.scalar.copy, 1)
+        weave(nc.scalar.copy, 2)
+        product(0)
+        weave(nc.vector.tensor_copy, 3)
+        for u in range(1, PACK):
+            product(u)
+        for u in range(PACK):
+            nc.scalar.activation(s_win[u][:, :S], s_ps[u][:], ACT.Copy, scale=0.0625)
+
+        chunks = ((0, 256), (256, 128), (384, 128))
+        units = ((0, 0, 2), (0, 2, 4), (1, 0, 4), (2, 0, 2), (2, 2, 4))
+
+        def staged(name, dtype=F32):
+            return [new("%s%d" % (name, c), [P, PACK, w], dtype) for c, (c0, w) in enumerate(chunks)]
+
+        res = staged("res")
+        pa = new("pa", [P, PACK, S], F32)
+        pa_sq = [new("pa_sq%d" % u, [P, S], F32) for u in range(PACK)]
+        root = [new("root%d" % i, [P, (u1 - u0) * chunks[c][1]], F32) for i, (c, u0, u1) in enumerate(units)]
+        inv = [new("inv%d" % i, [P, (u1 - u0) * chunks[c][1]], F32) for i, (c, u0, u1) in enumerate(units)]
+        inv_ps = {}
+        res_il = [new("res_il%d" % c, [P, w, PACK], BF16) for c, (c0, w) in enumerate(chunks)]
         res_w = new("res_w", [P, S], I32)
         res_s = new("res_s", [P, S], U8)
         out_rows = out_0.rearrange("(p t) c -> p t c", t=PACK)
         out_words = out_1[0].rearrange("p c r -> p (c r)").bitcast(I32)
 
-        def front(h, v):
-            us = slice(2 * v, 2 * v + 2)
-            for u in (2 * v, 2 * v + 1):
-                nc.scalar.activation(s_sq[h][:, u, :], s_ps[h][u][:], ACT.Square, scale=0.0625)
-            for u in (2 * v, 2 * v + 1):
-                nc.vector.tensor_copy(pa[h][:, u, :], s_win[u][:].indirect(lists["n5"][:, 16 * h : 16 * h + 16]))
-            nc.scalar.activation(pa_sq[h][:, us, :], pa[h][:, us, :], ACT.Square)
-            for u in (2 * v, 2 * v + 1):
-                nc.vector.scalar_tensor_tensor(num[h][:, u, :], s_ps[h][u][:], 0.125, pa[h][:, u, :], ALU.mult, ALU.mult)
+        def front(u):
+            nc.vector.tensor_copy(pa[:, u, :], s_win[u][:].indirect(lists["n5"][:]))
+            if u < PACK - 1:
+                nc.scalar.activation(s_sq[:, u, :], s_ps[u][:], ACT.Square, scale=0.0625)
+            else:
+                nc.vector.tensor_tensor(s_sq[:, u, :], s_win[u][:, :S], s_win[u][:, :S], ALU.mult)
+            nc.scalar.activation(pa_sq[u][:], pa[:, u, :], ACT.Square)
 
-        def middle(h, v):
-            us = slice(2 * v, 2 * v + 2)
-            nc.vector.scalar_tensor_tensor(den[h][:, us, :], s_sq[h][:, us, :], 0.5, pa_sq[h][:, us, :], ALU.add, ALU.add)
-            nc.scalar.activation(root[h][:, us, :], den[h][:, us, :], ACT.Abs_reciprocal_sqrt)
-            nc.scalar.activation(inv[h][:, us, :], root[h][:, us, :], ACT.Square)
+        def numerator(u):
+            nc.vector.scalar_tensor_tensor(pa[:, u, :], s_win[u][:, :S], 2.0, pa[:, u, :], ALU.mult, ALU.mult)
 
-        def back(h, v):
-            us = slice(2 * v, 2 * v + 2)
-            cols = slice(h * HALF, (h + 1) * HALF)
-            nc.vector.tensor_tensor(res[h][:, us, :], num[h][:, us, :], inv[h][:, us, :], ALU.mult)
-            nc.sync.dma_start(out_rows[:, us, cols], res[h][:, us, :])
-            if v == 1:
+        def middle(c, u0, u1):
+            c0, w = chunks[c]
+            i = units.index((c, u0, u1))
+            blocks = [(u, j0) for u in range(u0, u1) for j0 in range(0, w, P)]
+            den_ps = psum.tile([P, len(blocks), P], F32, name="den_ps%d" % i, tag="bank%d" % (6 + i % 2))
+            for b, (u, j0) in enumerate(blocks):
+                nc.tensor.matmul(den_ps[:, b, :], lhsT=s_sq[:, u, c0 + j0 : c0 + j0 + P], rhs=ident[:], is_transpose=True, start=True, stop=False)
+                nc.tensor.matmul(den_ps[:, b, :], lhsT=pa_sq[u][:, c0 + j0 : c0 + j0 + P], rhs=ident[:], is_transpose=True, start=False, stop=True)
+            nc.scalar.activation(root[i][:], den_ps[:].rearrange("j b p -> j (b p)"), ACT.Abs_reciprocal_sqrt, bias=0.5)
+            nc.scalar.activation(inv[i][:], root[i][:], ACT.Square)
+            inv_ps[i] = psum.tile([P, len(blocks) * P], F32, name="inv_ps%d" % i, tag="bank%d" % (i % 2))
+            for b in range(len(blocks)):
+                nc.tensor.transpose(inv_ps[i][:, b * P : (b + 1) * P], inv[i][:, b * P : (b + 1) * P], ident[:])
+
+        def back(c, u0, u1):
+            c0, w = chunks[c]
+            cols = slice(c0, c0 + w)
+            inverse = inv_ps[units.index((c, u0, u1))][:].rearrange("p (u w) -> p u w", w=w)
+            nc.vector.tensor_tensor(res[c][:, u0:u1, :], pa[:, u0:u1, cols], inverse, ALU.mult)
+            nc.sync.dma_start(out_rows[:, u0:u1, cols], res[c][:, u0:u1, :])
+            if u1 == PACK:
                 nc.vector.tensor_copy(
-                    res_il[h][:].rearrange("p (c i) t -> p c t i", i=4),
-                    res[h][:].rearrange("p t (c i) -> p c t i", i=4),
+                    res_il[c][:].rearrange("p (c i) t -> p c t i", i=4),
+                    res[c][:].rearrange("p t (c i) -> p c t i", i=4),
                 )
-                nc.vector.quantize_mx(res_w[:, cols].bitcast(FP8X4), res_s[:, cols], res_il[h][:].rearrange("p j t -> p (j t)"))
+                nc.vector.quantize_mx(res_w[:, cols].bitcast(FP8X4), res_s[:, cols], res_il[c][:].rearrange("p j t -> p (j t)"))
                 nc.sync.dma_start(out_words[:, cols], res_w[:, cols])
 
-        units = [(h, v) for h in range(2) for v in range(2)]
-        for i in range(len(units) + 2):
+        front(0)
+        front(1)
+        middle(*units[0])
+        front(2)
+        front(3)
+        for u in range(PACK):
+            numerator(u)
+        for i in range(1, len(units) + 1):
             if i < len(units):
-                front(*units[i])
-            if 1 <= i <= len(units):
-                middle(*units[i - 1])
-            if i >= 2:
-                back(*units[i - 2])
+                middle(*units[i])
+            back(*units[i - 1])
         for q in range(4):
             eng = nc.scalar if q % 2 else nc.sync
             eng.dma_start(out_2[0, 4 * q : 4 * q + 4, :].bitcast(I32), res_s[32 * q : 32 * q + 4, :].bitcast(I32))

from contextlib import ExitStack

import concourse.mybir as mybir
from concourse.masks import make_identity

F32 = mybir.dt.float32
BF16 = mybir.dt.bfloat16
I32 = mybir.dt.int32
U32 = mybir.dt.uint32
U16 = mybir.dt.uint16
U8 = mybir.dt.uint8
FP8X4 = mybir.dt.float8_e4m3fn_x4
ALU = mybir.AluOpType
ACT = mybir.ActivationFunctionType

P = 128
PACK = 4
T = 2048
S = 512
HALF = S // 2
WIDE = 2 * S
FLOPS = 2 * 2 * 512 * 512 * 512


def tile_picked_selfhopmxtrackharm_none_po_kernel(
    tc, x_words, x_scales, w1_words, w1_scales, ga, gb, offs, n1, n2, n3, n4, n5, out_0, out_1, out_2
):
    nc = tc.nc
    with ExitStack() as ctx:
        held = ctx.enter_context(tc.tile_pool(name="held", bufs=1))
        psum = ctx.enter_context(tc.psum_pool(name="psum", bufs=1))

        def new(name, shape, dtype, tag=""):
            return held.tile(shape, dtype, name=name, tag=tag or name, align_bytes=64)

        lists = {}
        for name in ("offs", "n1", "n2", "n3", "n4", "n5"):
            lists[name] = held.tile([P, S // 16], U16, name="list_" + name)

        xw = new("xw", [P, T], I32)
        xs = new("xs", [P, T], U8)
        ww = new("ww", [P, S], I32)
        ws = new("ws", [P, S], U8)
        ga_t = new("ga_t", [P, PACK], F32)
        gb_t = new("gb_t", [P, PACK], F32)
        warm_in = new("warm_in", [P, 1], F32)
        warm_a = new("warm_a", [P, 1], F32)
        warm_b = new("warm_b", [P, 1], F32)

        nc.gpsimd.memset(xs[:].bitcast(I32), 0)
        nc.gpsimd.memset(ws[:].bitcast(I32), 0)
        nc.vector.memset(warm_in[:], 0.0)

        def scale_rows(dst, src, queues):
            for q, eng in enumerate(queues):
                eng.dma_start(dst[32 * q : 32 * q + 4, :].bitcast(I32), src[0, 4 * q : 4 * q + 4, :].bitcast(I32))

        nc.scalar.dma_start(ga_t[:], ga.rearrange("(p t) o -> p (t o)", t=PACK))
        for name, src in (("offs", offs), ("n1", n1), ("n2", n2)):
            nc.sync.dma_start(lists[name][:], src)
        nc.sync.dma_start(xw[:], x_words[0].rearrange("p c r -> p (c r)").bitcast(I32))
        scale_rows(xs, x_scales, [nc.sync] * 4)
        scale_rows(ws, w1_scales, [nc.sync, nc.sync, nc.gpsimd, nc.gpsimd])
        nc.sync.dma_start(ww[:], w1_words[0].rearrange("p c r -> p (c r)").bitcast(I32))
        nc.sync.dma_start(gb_t[:], gb.rearrange("(p t) o -> p (t o)", t=PACK))
        for name, src in (("n3", n3), ("n4", n4), ("n5", n5)):
            nc.sync.dma_start(lists[name][:], src)
        nc.scalar.activation(warm_a[:], warm_in[:], ACT.Sigmoid)
        ident = new("ident", [P, P], F32)
        make_identity(nc, ident[:])

        xgw = new("xgw", [P, S], I32)
        xgs = new("xgs", [P, S], U8)
        wdw = [new("wdw%d" % t, [P, P], I32) for t in range(PACK)]
        wds = [new("wds%d" % t, [P, P], U8) for t in range(PACK)]
        flip = new("flip", [P, PACK], F32)
        aga = new("aga", [P, PACK], F32)
        ngb = new("ngb", [P, PACK], F32)
        nc.scalar.activation(aga[:], ga_t[:], ACT.Abs)
        ww_by_t = ww[:].bitcast(U32).rearrange("p (m t) -> p m t", t=PACK)
        ws_by_t = ws[:].rearrange("p (m t) -> p m t", t=PACK)
        nc.vector.tensor_copy(xgw[:].bitcast(U32), xw[:].bitcast(U32).indirect(lists["offs"][:]))
        nc.vector.tensor_copy(xgs[:, :HALF], xs[:].indirect(lists["offs"][:, :16]))
        nc.vector.tensor_copy(wdw[0][:].bitcast(U32), ww_by_t[:, :, 0])
        nc.vector.tensor_copy(wds[0][:], ws_by_t[:, :, 0])
        nc.vector.tensor_copy(xgs[:, HALF:], xs[:].indirect(lists["offs"][:, 16:]))
        for t in range(1, PACK):
            nc.vector.tensor_copy(wdw[t][:].bitcast(U32), ww_by_t[:, :, t])
            nc.vector.tensor_copy(wds[t][:], ws_by_t[:, :, t])
        nc.vector.tensor_scalar(flip[:], ga_t[:], 0.0, -2.0, ALU.is_ge, ALU.mult)
        nc.vector.scalar_tensor_tensor(ngb[:], flip[:], 1.0, gb_t[:], ALU.add, ALU.mult)

        y_parts = []
        for t in range(PACK):
            spans = ((slice(0, HALF), 0), (slice(HALF, S), PACK)) if t == 0 else ((slice(0, S), t),)
            parts = []
            for cols, bank in spans:
                acc = psum.tile([P, cols.stop - cols.start], F32, name="y_ps%d" % bank, tag="bank%d" % bank)
                nc.tensor.matmul_mx(
                    acc[:], lhsT=wdw[t][:].bitcast(FP8X4), lhsT_scale=wds[t][:],
                    rhs=xgw[:, cols].bitcast(FP8X4), rhs_scale=xgs[:, cols], start=True, stop=True,
                )
                parts.append((cols, acc))
            y_parts.append(parts)

        ya_win = [new("ya_win%d" % t, [P, WIDE], F32) for t in range(PACK)]
        y_win = [new("y_win%d" % t, [P, WIDE], F32) for t in range(PACK)]
        yb_win = [new("yb_win%d" % t, [P, WIDE], F32) for t in range(PACK)]
        st_win = [new("st_win%d" % t, [P, S], F32) for t in range(PACK)]
        ya = [new("ya%d" % t, [P, S], F32) for t in range(PACK)]
        st_hop = [[new("st_hop%d%d" % (t, h), [P, HALF], F32) for h in range(2)] for t in range(PACK)]
        gate = [new("gate%d" % t, [P, S], F32) for t in range(PACK)]
        far = [new("far%d" % t, [P, S], F32) for t in range(PACK)]
        near = [new("near%d" % t, [P, S], F32) for t in range(PACK)]
        z_planes = new("z_planes", [P, PACK, S], BF16)
        z2_turned = [new("z2_turned%d" % b, [P, 2, P, 2], BF16) for b in range(PACK)]
        z2_il = new("z2_il", [P, S, PACK], BF16)
        z_w = [new("z_w%d" % u, [P, P], U32) for u in range(PACK)]
        z_s = [new("z_s%d" % u, [P, P], U8) for u in range(PACK)]
        z2_w = new("z2_w", [P, S], U32)
        z2_s = new("z2_s", [P, S], U8)
        sum_ps = [psum.tile([P, PACK, P], F32, name="sum_ps%d" % b, tag="bank%d" % (PACK + b)) for b in range(PACK)]

        def evict_a(t):
            for cols, acc in y_parts[t]:
                nc.scalar.activation(ya_win[t][:, cols], acc[:], ACT.Copy, scale=aga[:, t : t + 1])
                nc.scalar.activation(ya[t][:, cols], acc[:], ACT.Copy, scale=aga[:, t : t + 1])

        def evict_b(t):
            for cols, acc in y_parts[t]:
                nc.scalar.copy(y_win[t][:, cols], acc[:])
            for cols, acc in y_parts[t]:
                nc.scalar.activation(yb_win[t][:, cols], acc[:], ACT.Copy, scale=ngb[:, t : t + 1])

        def make_gate(t):
            nc.scalar.activation(gate[t][:], y_win[t][:].indirect(lists["n3"][:]), ACT.Sigmoid)

        def step_a(t):
            nc.vector.tensor_tensor(st_win[t][:, :S], ya_win[t][:].indirect(lists["n1"][:]), ya[t][:], ALU.subtract)

        def step_b(t):
            for h in range(2):
                nc.vector.tensor_copy(st_hop[t][h][:], st_win[t][:].indirect(lists["n2"][:, 16 * h : 16 * h + 16]))

        def step_c(t):
            for h in range(2):
                cols = slice(h * HALF, (h + 1) * HALF)
                nc.vector.tensor_tensor(z_planes[:, t, cols], st_win[t][:, cols], st_hop[t][h][:], ALU.min)

        def step_d(t):
            nc.vector.tensor_tensor(far[t][:], yb_win[t][:].indirect(lists["n4"][:]), gate[t][:], ALU.mult)

        def step_e(t):
            nc.vector.scalar_tensor_tensor(near[t][:], gate[t][:], -1.0, yb_win[t][:, :S], ALU.mult, ALU.mult)
            terms = (yb_win[t], far[t], near[t])
            for i, term in enumerate(terms):
                for b in range(PACK):
                    nc.tensor.matmul(
                        sum_ps[b][:, t, :], lhsT=term[:, b * P : (b + 1) * P], rhs=ident[:],
                        is_transpose=True, start=(i == 0), stop=(i == len(terms) - 1),
                    )

        evict_a(0)
        evict_b(0)
        make_gate(0)
        evict_b(1)
        evict_a(1)
        make_gate(1)
        evict_b(2)
        make_gate(2)
        evict_b(3)
        evict_a(2)
        make_gate(3)
        evict_a(3)
        nc.scalar.activation(warm_b[:], ya[3][:, S - 1 : S], ACT.Abs_reciprocal_sqrt, scale=0.0, bias=1.0)
        step_a(0)
        step_b(0)
        step_c(0)
        step_d(0)
        step_e(0)
        step_a(1)
        step_d(1)
        step_b(1)
        step_e(1)
        step_c(1)
        step_d(2)
        step_e(2)
        step_a(2)
        step_d(3)
        step_e(3)
        step_b(2)
        step_a(3)
        step_c(2)
        step_b(3)

        back_ps = [psum.tile([P, 2, 2, P], F32, name="back_ps%d" % h, tag="bank%d" % h) for h in range(2)]
        for h in range(2):
            for b in (2 * h, 2 * h + 1):
                nc.scalar.copy(z2_turned[b][:], sum_ps[b][:].rearrange("j (u e) p -> j u p e", e=2))
                words = z2_turned[b][:].rearrange("j u p e -> j (u p e)").bitcast(F32)
                for u in range(2):
                    nc.tensor.transpose(back_ps[h][:, b % 2, u, :], words[:, u * P : (u + 1) * P], ident[:])
        for h in range(2):
            dst = z2_il[:, h * HALF : (h + 1) * HALF, :].rearrange("p j t -> p (j t)").bitcast(F32)
            nc.scalar.copy(dst.rearrange("p (b j u) -> p b j u", b=2, u=2), back_ps[h][:].rearrange("p b u j -> p b j u"))
        step_c(3)

        z_il = [new("z_il%d" % u, [P, P, PACK], BF16, tag="z2_turned3" if u == 1 else "z2_turned2" if u == 2 else "") for u in range(PACK)]

        def weave(copy, u):
            copy(
                z_il[u][:].rearrange("p (c i) t -> p c t i", i=4),
                z_planes[:].rearrange("p t (c i u) -> p u c t i", i=4, u=PACK)[:, u],
            )

        s_ps = [psum.tile([P, S], F32, name="s_ps%d" % u, tag="bank%d" % (2 + u)) for u in range(PACK)]
        s_win = [new("s_win%d" % u, [P, WIDE], F32) for u in range(PACK)]
        s_sq = new("s_sq", [P, PACK, S], F32)

        def product(u):
            nc.vector.quantize_mx(z_w[u][:].bitcast(FP8X4), z_s[u][:], z_il[u][:].rearrange("p m t -> p (m t)"))
            nc.tensor.matmul_mx(
                s_ps[u][:], lhsT=z_w[u][:].bitcast(FP8X4), lhsT_scale=z_s[u][:],
                rhs=z2_w[:].bitcast(FP8X4), rhs_scale=z2_s[:], start=True, stop=True,
            )

        weave(nc.vector.tensor_copy, 0)
        nc.vector.quantize_mx(z2_w[:].bitcast(FP8X4), z2_s[:], z2_il[:].rearrange("p j t -> p (j t)"))
        weave(nc.scalar.copy, 1)
        weave(nc.scalar.copy, 2)
        product(0)
        weave(nc.vector.tensor_copy, 3)
        for u in range(1, PACK):
            product(u)
        for u in range(PACK):
            nc.scalar.activation(s_win[u][:, :S], s_ps[u][:], ACT.Copy, scale=0.0625)

        chunks = ((0, 256), (256, 128), (384, 128))
        units = ((0, 0, 2), (0, 2, 4), (1, 0, 4), (2, 0, 2), (2, 2, 4))

        def staged(name, dtype=F32):
            return [new("%s%d" % (name, c), [P, PACK, w], dtype) for c, (c0, w) in enumerate(chunks)]

        res = staged("res")
        pa = new("pa", [P, PACK, S], F32)
        pa_sq = [new("pa_sq%d" % u, [P, S], F32) for u in range(PACK)]
        root = [new("root%d" % i, [P, (u1 - u0) * chunks[c][1]], F32) for i, (c, u0, u1) in enumerate(units)]
        inv = [new("inv%d" % i, [P, (u1 - u0) * chunks[c][1]], F32) for i, (c, u0, u1) in enumerate(units)]
        inv_ps = {}
        res_il = [new("res_il%d" % c, [P, w, PACK], BF16) for c, (c0, w) in enumerate(chunks)]
        res_w = new("res_w", [P, S], I32)
        res_s = new("res_s", [P, S], U8)
        out_rows = out_0.rearrange("(p t) c -> p t c", t=PACK)
        out_words = out_1[0].rearrange("p c r -> p (c r)").bitcast(I32)

        def front(u):
            nc.vector.tensor_copy(pa[:, u, :], s_win[u][:].indirect(lists["n5"][:]))
            if u < PACK - 1:
                nc.scalar.activation(s_sq[:, u, :], s_ps[u][:], ACT.Square, scale=0.0625)
            else:
                nc.vector.tensor_tensor(s_sq[:, u, :], s_win[u][:, :S], s_win[u][:, :S], ALU.mult)
            nc.scalar.activation(pa_sq[u][:], pa[:, u, :], ACT.Square)

        def numerator(u):
            nc.vector.scalar_tensor_tensor(pa[:, u, :], s_win[u][:, :S], 2.0, pa[:, u, :], ALU.mult, ALU.mult)

        def middle(c, u0, u1):
            c0, w = chunks[c]
            i = units.index((c, u0, u1))
            blocks = [(u, j0) for u in range(u0, u1) for j0 in range(0, w, P)]
            den_ps = psum.tile([P, len(blocks), P], F32, name="den_ps%d" % i, tag="bank%d" % (6 + i % 2))
            for b, (u, j0) in enumerate(blocks):
                nc.tensor.matmul(den_ps[:, b, :], lhsT=s_sq[:, u, c0 + j0 : c0 + j0 + P], rhs=ident[:], is_transpose=True, start=True, stop=False)
                nc.tensor.matmul(den_ps[:, b, :], lhsT=pa_sq[u][:, c0 + j0 : c0 + j0 + P], rhs=ident[:], is_transpose=True, start=False, stop=True)
            nc.scalar.activation(root[i][:], den_ps[:].rearrange("j b p -> j (b p)"), ACT.Abs_reciprocal_sqrt, bias=0.5)
            nc.scalar.activation(inv[i][:], root[i][:], ACT.Square)
            inv_ps[i] = psum.tile([P, len(blocks) * P], F32, name="inv_ps%d" % i, tag="bank%d" % (i % 2))
            for b in range(len(blocks)):
                nc.tensor.transpose(inv_ps[i][:, b * P : (b + 1) * P], inv[i][:, b * P : (b + 1) * P], ident[:])

        def back(c, u0, u1):
            c0, w = chunks[c]
            cols = slice(c0, c0 + w)
            inverse = inv_ps[units.index((c, u0, u1))][:].rearrange("p (u w) -> p u w", w=w)
            nc.vector.tensor_tensor(res[c][:, u0:u1, :], pa[:, u0:u1, cols], inverse, ALU.mult)
            nc.sync.dma_start(out_rows[:, u0:u1, cols], res[c][:, u0:u1, :])
            if u1 == PACK:
                nc.vector.tensor_copy(
                    res_il[c][:].rearrange("p (c i) t -> p c t i", i=4),
                    res[c][:].rearrange("p t (c i) -> p c t i", i=4),
                )
                nc.vector.quantize_mx(res_w[:, cols].bitcast(FP8X4), res_s[:, cols], res_il[c][:].rearrange("p j t -> p (j t)"))
                nc.sync.dma_start(out_words[:, cols], res_w[:, cols])

        front(0)
        front(1)
        middle(*units[0])
        front(2)
        front(3)
        for u in range(PACK):
            numerator(u)
        for i in range(1, len(units) + 1):
            if i < len(units):
                middle(*units[i])
            back(*units[i - 1])
        for q in range(4):
            eng = nc.scalar if q % 2 else nc.sync
            eng.dma_start(out_2[0, 4 * q : 4 * q + 4, :].bitcast(I32), res_s[32 * q : 32 * q + 4, :].bitcast(I32))
